import numpy as np
CORES = [32,33,34,35,288,289,290,291]
N = 8
def setup_inputs(rng):
    return {"x": rng.standard_normal((N, 128, 128), dtype=np.float32)}
def reference(x):
    s = x.sum(axis=0, dtype=np.float64).astype(x.dtype)
    return {"y": np.broadcast_to(s, (N,) + s.shape)}

@@ -1,0 +1,43 @@
+from concourse.bass import DstId, RemoteDMATransfer
+
+NP = 8
+SCRATCH = {
+    "a": ("dram", [NP, 128, 16], "float32"),
+    "b": ("dram", [NP, 128, 16], "float32"),
+}
+SEMAPHORES = ["loaded", "sent", "arrived", "ret1", "ret3", "st1", "st3"]
+
+HELPERS = [128 + 32 + c for c in (0, 2, 4, 6)] + [384 + 32 + c for c in (0, 2, 4, 6)]
+
+
+def rank_program(g, core, T, topo):
+    rank = T.rank_of(core)
+    S = T.sem
+    if rank is not None:
+        g.sync.dma_start(T.a[:], T.x[:]).then_inc(S.loaded, 16)
+        g.wait_ge(S.loaded, 16)
+        trs = []
+        for k, h in enumerate(HELPERS):
+            rid, pid = topo.addr(h, core)
+            trs.append(RemoteDMATransfer(dst_ids=[DstId(rid=rid, pnc=pid)], dma_engine_mask=1 << k,
+                                         remote_sem=S.arrived, src=T.a[k], dst=T.a[rank]))
+        g.remote_dma_fused(trs, local_sem=S.sent)
+        g.sync.wait_ge(S.ret1, 32)
+        g.sync.dma_start(T.y[0:64, :], T.b[0:4]).then_inc(S.st1, 16)
+        g.scalar.wait_ge(S.ret3, 32)
+        g.scalar.dma_start(T.y[64:128, :], T.b[4:8]).then_inc(S.st3, 16)
+        g.wait_ge(S.sent, NP)
+        g.sync.wait_ge(S.st1, 16)
+        g.scalar.wait_ge(S.st3, 16)
+        return
+    if core in HELPERS:
+        k = HELPERS.index(core)
+        ids = []
+        for r in T.cores:
+            rid, pid = topo.addr(r, core)
+            ids.append(DstId(rid=rid, pnc=pid))
+        g.wait_ge(S.arrived, len(T.cores))
+        tr = RemoteDMATransfer(dst_ids=ids, dma_engine_mask=0xFF, remote_sem=(S.ret1 if k < 4 else S.ret3),
+                               srcs=[T.a[r] for r in range(len(T.cores))], dsts=[T.b[k] for _ in T.cores], alu_op=1)
+        g.remote_dma_fused([tr], local_sem=S.sent)
+        g.wait_ge(S.sent, 8)

@@ -3,9 +3,10 @@ from concourse.bass import DstId, RemoteDMATransfer
 NP = 8
 SCRATCH = {
     "a": ("dram", [NP, 128, 16], "float32"),
+    "c": ("dram", [NP, 128, 16], "float32"),
     "b": ("dram", [NP, 128, 16], "float32"),
 }
-SEMAPHORES = ["loaded", "sent", "arrived", "ret1", "ret3", "st1", "st3"]
+SEMAPHORES = ["loaded", "sent", "rs", "arrived", "ret1", "ret3", "st1", "st3"]
 
 HELPERS = [128 + 32 + c for c in (0, 2, 4, 6)] + [384 + 32 + c for c in (0, 2, 4, 6)]
 
@@ -14,19 +15,32 @@ def rank_program(g, core, T, topo):
     rank = T.rank_of(core)
     S = T.sem
     if rank is not None:
+        li, grp = rank % 4, rank // 4
         g.sync.dma_start(T.a[:], T.x[:]).then_inc(S.loaded, 16)
         g.wait_ge(S.loaded, 16)
         trs = []
-        for k, h in enumerate(HELPERS):
-            rid, pid = topo.addr(h, core)
-            trs.append(RemoteDMATransfer(dst_ids=[DstId(rid=rid, pnc=pid)], dma_engine_mask=1 << k,
-                                         remote_sem=S.arrived, src=T.a[k], dst=T.a[rank]))
+        for pj in range(4):
+            if pj == li:
+                continue
+            rid, pid = topo.addr(T.cores[4 * grp + pj], core)
+            for s in range(2):
+                trs.append(RemoteDMATransfer(dst_ids=[DstId(rid=rid, pnc=pid)], dma_engine_mask=3 << (2 * len(trs)),
+                                             remote_sem=S.rs, src=T.a[pj + 4 * s], dst=T.c[2 * li + s]))
+        g.remote_dma_fused(trs, local_sem=S.sent)
+        g.wait_ge(S.rs, 12)
+        trs = []
+        for s in range(2):
+            rid, pid = topo.addr(HELPERS[li + 4 * s], core)
+            trs.append(RemoteDMATransfer(dst_ids=[DstId(rid=rid, pnc=pid)], dma_engine_mask=0xF << (4 * s),
+                                         remote_sem=S.arrived,
+                                         srcs=[T.a[li + 4 * s]] + [T.c[2 * i + s] for i in range(4) if i != li],
+                                         dsts=[T.c[grp]], alu_op=1))
         g.remote_dma_fused(trs, local_sem=S.sent)
         g.sync.wait_ge(S.ret1, 32)
         g.sync.dma_start(T.y[0:64, :], T.b[0:4]).then_inc(S.st1, 16)
         g.scalar.wait_ge(S.ret3, 32)
         g.scalar.dma_start(T.y[64:128, :], T.b[4:8]).then_inc(S.st3, 16)
-        g.wait_ge(S.sent, NP)
+        g.wait_ge(S.sent, 20)
         g.sync.wait_ge(S.st1, 16)
         g.scalar.wait_ge(S.st3, 16)
         return
@@ -36,8 +50,8 @@ def rank_program(g, core, T, topo):
         for r in T.cores:
             rid, pid = topo.addr(r, core)
             ids.append(DstId(rid=rid, pnc=pid))
-        g.wait_ge(S.arrived, len(T.cores))
+        g.wait_ge(S.arrived, 8)
         tr = RemoteDMATransfer(dst_ids=ids, dma_engine_mask=0xFF, remote_sem=(S.ret1 if k < 4 else S.ret3),
-                               srcs=[T.a[r] for r in range(len(T.cores))], dsts=[T.b[k] for _ in T.cores], alu_op=1)
+                               srcs=[T.c[0], T.c[1]], dsts=[T.b[k] for _ in T.cores], alu_op=1)
         g.remote_dma_fused([tr], local_sem=S.sent)
         g.wait_ge(S.sent, 8)

@@ -1,14 +1,19 @@
 from concourse.bass import DstId, RemoteDMATransfer
 
-NP = 8
+NP = 4
 SCRATCH = {
-    "a": ("dram", [NP, 128, 16], "float32"),
-    "c": ("dram", [NP, 128, 16], "float32"),
-    "b": ("dram", [NP, 128, 16], "float32"),
+    "a": ("dram", [NP, 128, 32], "float32"),
+    "c": ("dram", [NP, 128, 32], "float32"),
+    "b": ("dram", [NP, 128, 32], "float32"),
 }
-SEMAPHORES = ["loaded", "sent", "rs", "arrived", "ret1", "ret3", "st1", "st3"]
+SEMAPHORES = ["loaded", "sent", "rs", "arrived", "ret", "ag", "st1", "st3"]
 
-HELPERS = [128 + 32 + c for c in (0, 2, 4, 6)] + [384 + 32 + c for c in (0, 2, 4, 6)]
+HELPERS = [128 + 32 + 0, 384 + 32 + 0, 128 + 32 + 4, 384 + 32 + 4]
+
+
+def _dst(topo, d, core):
+    rid, pid = topo.addr(d, core)
+    return DstId(rid=rid, pnc=pid)
 
 
 def rank_program(g, core, T, topo):
@@ -16,42 +21,39 @@ def rank_program(g, core, T, topo):
     S = T.sem
     if rank is not None:
         li, grp = rank % 4, rank // 4
+        peers = [i for i in range(4) if i != li]
         g.sync.dma_start(T.a[:], T.x[:]).then_inc(S.loaded, 16)
         g.wait_ge(S.loaded, 16)
-        trs = []
-        for pj in range(4):
-            if pj == li:
-                continue
-            rid, pid = topo.addr(T.cores[4 * grp + pj], core)
-            for s in range(2):
-                trs.append(RemoteDMATransfer(dst_ids=[DstId(rid=rid, pnc=pid)], dma_engine_mask=3 << (2 * len(trs)),
-                                             remote_sem=S.rs, src=T.a[pj + 4 * s], dst=T.c[2 * li + s]))
-        g.remote_dma_fused(trs, local_sem=S.sent)
+        g.remote_dma_fused(
+            [RemoteDMATransfer(dst_ids=[_dst(topo, T.cores[4 * grp + pj], core)], dma_engine_mask=0xF << (4 * n),
+                               remote_sem=S.rs, src=T.a[pj], dst=T.c[li]) for n, pj in enumerate(peers)],
+            local_sem=S.sent)
         g.wait_ge(S.rs, 12)
-        trs = []
-        for s in range(2):
-            rid, pid = topo.addr(HELPERS[li + 4 * s], core)
-            trs.append(RemoteDMATransfer(dst_ids=[DstId(rid=rid, pnc=pid)], dma_engine_mask=0xF << (4 * s),
-                                         remote_sem=S.arrived,
-                                         srcs=[T.a[li + 4 * s]] + [T.c[2 * i + s] for i in range(4) if i != li],
-                                         dsts=[T.c[grp]], alu_op=1))
-        g.remote_dma_fused(trs, local_sem=S.sent)
-        g.sync.wait_ge(S.ret1, 32)
-        g.sync.dma_start(T.y[0:64, :], T.b[0:4]).then_inc(S.st1, 16)
-        g.scalar.wait_ge(S.ret3, 32)
-        g.scalar.dma_start(T.y[64:128, :], T.b[4:8]).then_inc(S.st3, 16)
-        g.wait_ge(S.sent, 20)
+        g.remote_dma_fused(
+            [RemoteDMATransfer(dst_ids=[_dst(topo, HELPERS[li], core)], dma_engine_mask=0xFF, remote_sem=S.arrived,
+                               srcs=[T.a[li]] + [T.c[i] for i in peers], dsts=[T.c[grp]], alu_op=1)],
+            local_sem=S.sent)
+        g.wait_ge(S.ret, 8)
+        g.remote_dma_fused(
+            [RemoteDMATransfer(dst_ids=[_dst(topo, T.cores[4 * grp + pj], core) for pj in peers], dma_engine_mask=0xFFFF,
+                               remote_sem=S.ag, srcs=[T.b[li]], dsts=[T.b[li] for _ in peers])],
+            local_sem=S.sent)
+        g.sync.wait_ge(S.ret, 8)
+        g.sync.wait_ge(S.ag, 48)
+        g.sync.dma_start(T.y[0:64, :], T.b[0:2]).then_inc(S.st1, 16)
+        g.scalar.wait_ge(S.ret, 8)
+        g.scalar.wait_ge(S.ag, 48)
+        g.scalar.dma_start(T.y[64:128, :], T.b[2:4]).then_inc(S.st3, 16)
+        g.wait_ge(S.sent, 36)
         g.sync.wait_ge(S.st1, 16)
         g.scalar.wait_ge(S.st3, 16)
         return
     if core in HELPERS:
         k = HELPERS.index(core)
-        ids = []
-        for r in T.cores:
-            rid, pid = topo.addr(r, core)
-            ids.append(DstId(rid=rid, pnc=pid))
-        g.wait_ge(S.arrived, 8)
-        tr = RemoteDMATransfer(dst_ids=ids, dma_engine_mask=0xFF, remote_sem=(S.ret1 if k < 4 else S.ret3),
-                               srcs=[T.c[0], T.c[1]], dsts=[T.b[k] for _ in T.cores], alu_op=1)
-        g.remote_dma_fused([tr], local_sem=S.sent)
+        g.wait_ge(S.arrived, 16)
+        g.remote_dma_fused(
+            [RemoteDMATransfer(dst_ids=[_dst(topo, T.cores[k], core), _dst(topo, T.cores[4 + k], core)],
+                               dma_engine_mask=0xFF, remote_sem=S.ret, srcs=[T.c[0], T.c[1]], dsts=[T.b[k], T.b[k]],
+                               alu_op=1)],
+            local_sem=S.sent)
         g.wait_ge(S.sent, 8)

@@ -1,14 +1,15 @@
 from concourse.bass import DstId, RemoteDMATransfer
 
-NP = 4
+NP = 8
 SCRATCH = {
-    "a": ("dram", [NP, 128, 32], "float32"),
-    "c": ("dram", [NP, 128, 32], "float32"),
-    "b": ("dram", [NP, 128, 32], "float32"),
+    "a": ("dram", [NP, 128, 16], "float32"),
+    "c": ("dram", [4, 128, 16], "float32"),
+    "b": ("dram", [NP, 128, 16], "float32"),
 }
-SEMAPHORES = ["loaded", "sent", "rs", "arrived", "ret", "ag", "st1", "st3"]
+SEMAPHORES = ["loaded", "sent", "rs", "arrived", "ret", "ag1", "ag0", "st1", "st0"]
 
-HELPERS = [128 + 32 + 0, 384 + 32 + 0, 128 + 32 + 4, 384 + 32 + 4]
+BASE = [32, 288]
+HELPERS = [(128 if p % 2 == 0 else 384) + 32 + p for p in range(NP)]
 
 
 def _dst(topo, d, core):
@@ -17,43 +18,59 @@ def _dst(topo, d, core):
 
 
 def rank_program(g, core, T, topo):
-    rank = T.rank_of(core)
     S = T.sem
-    if rank is not None:
-        li, grp = rank % 4, rank // 4
-        peers = [i for i in range(4) if i != li]
-        g.sync.dma_start(T.a[:], T.x[:]).then_inc(S.loaded, 16)
-        g.wait_ge(S.loaded, 16)
-        g.remote_dma_fused(
-            [RemoteDMATransfer(dst_ids=[_dst(topo, T.cores[4 * grp + pj], core)], dma_engine_mask=0xF << (4 * n),
-                               remote_sem=S.rs, src=T.a[pj], dst=T.c[li]) for n, pj in enumerate(peers)],
-            local_sem=S.sent)
-        g.wait_ge(S.rs, 12)
-        g.remote_dma_fused(
-            [RemoteDMATransfer(dst_ids=[_dst(topo, HELPERS[li], core)], dma_engine_mask=0xFF, remote_sem=S.arrived,
-                               srcs=[T.a[li]] + [T.c[i] for i in peers], dsts=[T.c[grp]], alu_op=1)],
-            local_sem=S.sent)
-        g.wait_ge(S.ret, 8)
-        g.remote_dma_fused(
-            [RemoteDMATransfer(dst_ids=[_dst(topo, T.cores[4 * grp + pj], core) for pj in peers], dma_engine_mask=0xFFFF,
-                               remote_sem=S.ag, srcs=[T.b[li]], dsts=[T.b[li] for _ in peers])],
-            local_sem=S.sent)
-        g.sync.wait_ge(S.ret, 8)
-        g.sync.wait_ge(S.ag, 48)
-        g.sync.dma_start(T.y[0:64, :], T.b[0:2]).then_inc(S.st1, 16)
-        g.scalar.wait_ge(S.ret, 8)
-        g.scalar.wait_ge(S.ag, 48)
-        g.scalar.dma_start(T.y[64:128, :], T.b[2:4]).then_inc(S.st3, 16)
-        g.wait_ge(S.sent, 36)
-        g.sync.wait_ge(S.st1, 16)
-        g.scalar.wait_ge(S.st3, 16)
-        return
     if core in HELPERS:
-        k = HELPERS.index(core)
+        p = HELPERS.index(core)
         g.wait_ge(S.arrived, 16)
         g.remote_dma_fused(
-            [RemoteDMATransfer(dst_ids=[_dst(topo, T.cores[k], core), _dst(topo, T.cores[4 + k], core)],
-                               dma_engine_mask=0xFF, remote_sem=S.ret, srcs=[T.c[0], T.c[1]], dsts=[T.b[k], T.b[k]],
+            [RemoteDMATransfer(dst_ids=[_dst(topo, BASE[0] + p, core), _dst(topo, BASE[1] + p, core)],
+                               dma_engine_mask=0xFF, remote_sem=S.ret, srcs=[T.c[0], T.c[1]], dsts=[T.b[p], T.b[p]],
                                alu_op=1)],
             local_sem=S.sent)
         g.wait_ge(S.sent, 8)
+        return
+    if core - BASE[0] in range(NP):
+        grp = 0
+    elif core - BASE[1] in range(NP):
+        grp = 1
+    else:
+        return
+    p = core - BASE[grp]
+    is_rank = p < 4
+    sent = 0
+    if is_rank:
+        g.sync.dma_start(T.a[:], T.x[:]).then_inc(S.loaded, 16)
+        g.wait_ge(S.loaded, 16)
+        out = [q for q in range(NP) if q != p]
+        g.remote_dma_fused(
+            [RemoteDMATransfer(dst_ids=[_dst(topo, BASE[grp] + q, core)], dma_engine_mask=3 << (2 * n),
+                               remote_sem=S.rs, src=T.a[q], dst=T.c[p]) for n, q in enumerate(out)],
+            local_sem=S.sent)
+        sent += 14
+        g.wait_ge(S.rs, 6)
+        srcs = [T.a[p]] + [T.c[i] for i in range(4) if i != p]
+    else:
+        g.wait_ge(S.rs, 8)
+        srcs = [T.c[i] for i in range(4)]
+    g.remote_dma_fused(
+        [RemoteDMATransfer(dst_ids=[_dst(topo, HELPERS[p], core)], dma_engine_mask=0xFF, remote_sem=S.arrived,
+                           srcs=srcs, dsts=[T.c[grp]], alu_op=1)],
+        local_sem=S.sent)
+    sent += 8
+    g.wait_ge(S.ret, 8)
+    to = [i for i in range(4) if i != p]
+    g.remote_dma_fused(
+        [RemoteDMATransfer(dst_ids=[_dst(topo, BASE[grp] + i, core) for i in to], dma_engine_mask=0xFFFF,
+                           remote_sem=(S.ag1 if is_rank else S.ag0), srcs=[T.b[p]], dsts=[T.b[p] for _ in to])],
+        local_sem=S.sent)
+    sent += 16
+    if is_rank:
+        g.sync.wait_ge(S.ret, 8)
+        g.sync.wait_ge(S.ag1, 48)
+        g.sync.dma_start(T.y[0:64, :], T.b[0:4]).then_inc(S.st1, 16)
+        g.scalar.wait_ge(S.ag0, 64)
+        g.scalar.dma_start(T.y[64:128, :], T.b[4:8]).then_inc(S.st0, 16)
+    g.wait_ge(S.sent, sent)
+    if is_rank:
+        g.sync.wait_ge(S.st1, 16)
+        g.scalar.wait_ge(S.st0, 16)

from concourse.bass import DstId, RemoteDMATransfer

NP = 8
SCRATCH = {
    "a": ("dram", [NP, 128, 16], "float32"),
    "c": ("dram", [4, 128, 16], "float32"),
    "b": ("dram", [NP, 128, 16], "float32"),
}
SEMAPHORES = ["loaded", "sent", "rs", "arrived", "ret", "ag1", "ag0", "st1", "st0"]

BASE = [32, 288]
HELPERS = [(128 if p % 2 == 0 else 384) + 32 + p for p in range(NP)]


def _dst(topo, d, core):
    rid, pid = topo.addr(d, core)
    return DstId(rid=rid, pnc=pid)


def rank_program(g, core, T, topo):
    S = T.sem
    if core in HELPERS:
        p = HELPERS.index(core)
        g.wait_ge(S.arrived, 16)
        g.remote_dma_fused(
            [RemoteDMATransfer(dst_ids=[_dst(topo, BASE[0] + p, core), _dst(topo, BASE[1] + p, core)],
                               dma_engine_mask=0xFF, remote_sem=S.ret, srcs=[T.c[0], T.c[1]], dsts=[T.b[p], T.b[p]],
                               alu_op=1)],
            local_sem=S.sent)
        g.wait_ge(S.sent, 8)
        return
    if core - BASE[0] in range(NP):
        grp = 0
    elif core - BASE[1] in range(NP):
        grp = 1
    else:
        return
    p = core - BASE[grp]
    is_rank = p < 4
    sent = 0
    if is_rank:
        g.sync.dma_start(T.a[:], T.x[:]).then_inc(S.loaded, 16)
        g.wait_ge(S.loaded, 16)
        out = [q for q in range(NP) if q != p]
        g.remote_dma_fused(
            [RemoteDMATransfer(dst_ids=[_dst(topo, BASE[grp] + q, core)], dma_engine_mask=3 << (2 * n),
                               remote_sem=S.rs, src=T.a[q], dst=T.c[p]) for n, q in enumerate(out)],
            local_sem=S.sent)
        sent += 14
        g.wait_ge(S.rs, 6)
        srcs = [T.a[p]] + [T.c[i] for i in range(4) if i != p]
    else:
        g.wait_ge(S.rs, 8)
        srcs = [T.c[i] for i in range(4)]
    g.remote_dma_fused(
        [RemoteDMATransfer(dst_ids=[_dst(topo, HELPERS[p], core)], dma_engine_mask=0xFF, remote_sem=S.arrived,
                           srcs=srcs, dsts=[T.c[grp]], alu_op=1)],
        local_sem=S.sent)
    sent += 8
    g.wait_ge(S.ret, 8)
    to = [i for i in range(4) if i != p]
    g.remote_dma_fused(
        [RemoteDMATransfer(dst_ids=[_dst(topo, BASE[grp] + i, core) for i in to], dma_engine_mask=0xFFFF,
                           remote_sem=(S.ag1 if is_rank else S.ag0), srcs=[T.b[p]], dsts=[T.b[p] for _ in to])],
        local_sem=S.sent)
    sent += 16
    if is_rank:
        g.sync.wait_ge(S.ret, 8)
        g.sync.wait_ge(S.ag1, 48)
        g.sync.dma_start(T.y[0:64, :], T.b[0:4]).then_inc(S.st1, 16)
        g.scalar.wait_ge(S.ag0, 64)
        g.scalar.dma_start(T.y[64:128, :], T.b[4:8]).then_inc(S.st0, 16)
    g.wait_ge(S.sent, sent)
    if is_rank:
        g.sync.wait_ge(S.st1, 16)
        g.scalar.wait_ge(S.st0, 16)
